import numpy as np
import ml_dtypes


def mxq(x, axis, fmt="e4m3"):
    dtype, down = {"e4m3": (ml_dtypes.float8_e4m3fn, 7), "e5m2": (ml_dtypes.float8_e5m2, 14)}[fmt]
    v = np.moveaxis(np.asarray(x, np.float32).astype(ml_dtypes.bfloat16).astype(np.float64), axis, -1)
    blocks = v.reshape(v.shape[:-1] + (-1, 32))
    amax = np.abs(blocks).max(-1, keepdims=True)
    byte = np.maximum(np.where(amax > 0, np.frexp(amax)[1] - 1 + 127, 0) - down, 1)
    scale = np.exp2(byte - 127.0)
    codes = (blocks / scale).astype(np.float32).astype(dtype).astype(np.float64)
    return np.moveaxis((codes * scale).reshape(v.shape), -1, axis)


WIDE = False


def mx_kscale(k):
    if not WIDE:
        return np.ones(k)
    levels = np.array([10, -10, 5, -5, 0])
    if k % 512:
        return np.exp2(np.random.permutation(np.resize(levels, k // 32))).repeat(32)
    a = np.empty((k // 512, 16))
    for p in range(k // 512):
        a[p, :8] = np.random.permutation(np.resize(levels, 8))
        for g in range(8):
            far = levels[np.abs(levels - a[p, g]) >= 10]
            a[p, g + 8] = far[np.random.randint(len(far))]
    return np.exp2(a.ravel()).repeat(32)


def f64(x):
    return np.asarray(x).astype(np.float64)


def striped(idx):
    return np.tile(idx.reshape(-1, 16).T, (8, 1)).astype(np.uint16)


def unstriped(offs):
    return offs[:16].T.reshape(-1).astype(np.int64)


def striped8(idx):
    return np.concatenate([x.reshape(-1, 16).T for x in idx]).astype(np.uint16)


def runs(offs, k):
    lists = np.stack([offs[16 * r : 16 * r + 16].T.reshape(-1) for r in range(8)]).astype(np.int64)
    return lists[np.arange(k) % 512 // 64]


def pack_weight(w):
    k, n = w.shape
    w = f64(np.asarray(w, np.float32).astype(ml_dtypes.bfloat16)).reshape(k // 32, 32, n)
    amax = np.abs(w).max(1)
    byte = np.clip(np.where(amax > 0, np.frexp(amax)[1] - 1 + 127 - 7, 1), 1, 254)
    scaled = (w * np.exp2(127.0 - byte)[:, None, :]).reshape(k, n).astype(np.float32)
    words = np.ascontiguousarray(scaled.reshape(k // 512, 128, 4, n).transpose(0, 1, 3, 2)).astype(ml_dtypes.float8_e4m3fn).view(np.uint8)
    return words, np.ascontiguousarray(byte.astype(np.uint8).reshape(k // 512, 16, n))


def unpack_weight(words, scales):
    g, p, n, _ = words.shape
    vals = np.ascontiguousarray(words).view(ml_dtypes.float8_e4m3fn).astype(np.float64) * np.repeat(np.exp2(scales.astype(np.float64) - 127.0), 8, axis=1)[..., None]
    return vals.transpose(0, 1, 3, 2).reshape(g * 512, n)


def sigmoid(v):
    return 1.0 / (1.0 + np.exp(-np.maximum(v, -700.0)))

def planes(y):
    n, m = y.shape
    v = y.astype(np.float32).astype(ml_dtypes.bfloat16).astype(np.float64).reshape(n // 32, 32, m)
    top = np.abs(v).max(1)
    byte = np.clip(np.where(top > 0, np.frexp(top)[1] - 1 + 127 - 7, 1), 1, 254)
    codes = (v * np.exp2(127.0 - byte)[:, None, :]).reshape(n, m).astype(np.float32).astype(ml_dtypes.float8_e4m3fn).view(np.uint8)
    words = codes.reshape(n // 512, 128, 4, m).transpose(0, 1, 3, 2)
    return np.ascontiguousarray(words), np.ascontiguousarray(byte.astype(np.uint8).reshape(n // 512, 16, m))


K, T, S, N, H, W = 512, 2048, 512, 512, 512, 2048


def setup_inputs():
    n = np.random.standard_normal
    s = mx_kscale(K)[:, None]
    u = mx_kscale(S)
    packed_xT = pack_weight(n((K, T)) * s)
    return {
        "x_words": packed_xT[0],
        "x_scales": packed_xT[1],
        "wa": (n((K, H)) / np.sqrt(K) / s).astype(np.float32),
        "wb": (n((K, N)) / np.sqrt(K) / s).astype(np.float32),
        "gt": (np.random.uniform(0.5, 1.5, (S, 1)) * u[:, None]).astype(np.float32),
        "gi": (np.random.uniform(0.5, 1.5, (S, 1)) / u[:, None]).astype(np.float32),
        "offs": striped(np.random.permutation(T)[:S]),
        "two": striped(np.random.permutation(T)[:S]),
        "n1": striped(np.random.randint(0, H, W)),
        "n2": striped(np.random.permutation(N)),
        "n3": striped(np.random.permutation(N)),
        "n4": striped8(np.stack([np.random.permutation(N) for _ in range(8)])),
        "n5": striped8(np.stack([np.random.permutation(N) for _ in range(8)])),
    }


def reference(x_words, x_scales, wa, wb, gt, gi, offs, two, n1, n2, n3, n4, n5):
    xq = unpack_weight(x_words, x_scales)[:, unstriped(offs)]
    a = xq.T @ mxq(f64(wa), 0, "e4m3")
    mb = a[:, unstriped(n1)]
    ms = mb.reshape(S, H, 4).sum(axis=2)
    z = f64(gt) * (a * sigmoid(ms))
    x_two = unpack_weight(x_words, x_scales)[:, unstriped(two)]
    b = x_two.T @ mxq(f64(wb), 0, "e4m3")
    ex = np.exp(b)
    z2 = f64(gi) * (np.log(ex + ex[:, unstriped(n2)]) - b[:, unstriped(n3)])
    cv = 0.0625 * ((mxq(z, 0, "e4m3").T @ mxq(z2, 0, "e4m3")))
    out_0 = np.maximum(cv[np.arange(H)[:, None], runs(n4, H)], cv[np.arange(H)[:, None], runs(n5, H)]) - (0.75 * cv)
    return (out_0,) + planes(out_0)

@@ -1,0 +1,263 @@
+from contextlib import ExitStack
+
+import concourse.mybir as mybir
+
+K, T, S, N, H = 512, 2048, 512, 512, 512
+FLOPS = 3 * 2 * 512 * 512 * 512
+
+F32 = mybir.dt.float32
+BF16 = mybir.dt.bfloat16
+I32 = mybir.dt.int32
+U32 = mybir.dt.uint32
+U16 = mybir.dt.uint16
+U8 = mybir.dt.uint8
+FP8X4 = mybir.dt.float8_e4m3fn_x4
+ACT = mybir.ActivationFunctionType
+ALU = mybir.AluOpType
+AX = mybir.AxisListType
+
+P = 128
+PACK = 4
+LIST_ROWS = 16
+SPARE = 16
+MEMBER_RUN = 1024
+MEMBERS = 4
+WA_FIRST = 128
+WA_SPLIT = 384
+WA_PARTS = ((0, WA_FIRST), (WA_FIRST, WA_SPLIT), (WA_SPLIT, H))
+Z2_CHUNKS = ((0, 256), (256, 384), (384, 512))
+OUT_CHUNKS = ((0, 256), (256, 384), (384, 512))
+
+
+def tile_picked_mombgsumglseover_none_po_kernel(
+    tc, x_words, x_scales, wa, wb, gt, gi, offs, two, n1, n2, n3, n4, n5, out_0, out_1, out_2
+):
+    nc = tc.nc
+
+    with ExitStack() as ctx:
+        lists = ctx.enter_context(tc.tile_pool(name="lists", bufs=1))
+        sb = ctx.enter_context(tc.tile_pool(name="sb", bufs=1))
+        psum = ctx.enter_context(tc.psum_pool(name="psum", bufs=1))
+
+        def load_list(name, src):
+            tile = lists.tile(list(src.shape), U16, name=name)
+            nc.sync.dma_start(tile[:], src)
+            return tile
+
+        def entries(tile, lo, hi):
+            return tile[:, lo // LIST_ROWS : hi // LIST_ROWS]
+
+        def weave(engine_copy, grouped, planes):
+            engine_copy(
+                grouped.rearrange("p (c i t) -> p c t i", i=4, t=PACK),
+                planes.rearrange("p t (c i) -> p c t i", i=4),
+            )
+
+        def interleave(engine_copy, name, planes, width, tag=None):
+            grouped = sb.tile([P, width * PACK], BF16, name=name, tag=tag or name, align_bytes=64)
+            weave(engine_copy, grouped[:], planes)
+            return grouped
+
+        def quantize(grouped, codes, scales):
+            nc.vector.quantize_mx(out=codes.bitcast(FP8X4), scales=scales, in_=grouped[:])
+
+        def product(out, lhs_codes, lhs_scales, rhs_codes, rhs_scales):
+            nc.tensor.matmul_mx(
+                out=out,
+                lhsT=lhs_codes.bitcast(FP8X4),
+                lhsT_scale=lhs_scales,
+                rhs=rhs_codes.bitcast(FP8X4),
+                rhs_scale=rhs_scales,
+                start=True,
+                stop=True,
+            )
+
+        x_scale_rows = sb.tile([P, T], U8, name="x_scale_rows")
+        nc.vector.memset(x_scale_rows[:].bitcast(I32), 0)
+        offs_t = load_list("offs_t", offs)
+        wa_rows = wa.rearrange("(p j) c -> p j c", j=PACK)
+        wa_raw = [
+            sb.tile([P, PACK, hi - lo], F32, name=f"wa_raw{lo}", tag=f"wa_raw{lo}", align_bytes=64)
+            for lo, hi in WA_PARTS
+        ]
+        nc.sync.dma_start(wa_raw[0][:], wa_rows[:, :, :WA_FIRST])
+        for q in range(4):
+            nc.sync.dma_start(
+                x_scale_rows[32 * q : 32 * q + 4, :].bitcast(I32), x_scales[0][4 * q : 4 * q + 4, :].bitcast(I32)
+            )
+        nc.sync.dma_start(wa_raw[1][:], wa_rows[:, :, WA_FIRST:WA_SPLIT])
+        x_word_table = sb.tile([P, T], U32, name="x_word_table")
+        nc.sync.dma_start(x_word_table[:].bitcast(I32), x_words[0].rearrange("p n t -> p (n t)").bitcast(I32))
+        nc.sync.dma_start(wa_raw[2][:], wa_rows[:, :, WA_SPLIT:])
+        n1_t = load_list("n1_t", n1)
+        wb_raw = sb.tile([P, PACK, N], F32, name="wb_raw")
+        nc.sync.dma_start(wb_raw[:], wb.rearrange("(p j) c -> p j c", j=PACK))
+        two_t = load_list("two_t", two)
+        gt_t = sb.tile([P, PACK], F32, name="gt_t")
+        nc.sync.dma_start(gt_t[:], gt.rearrange("(p t) o -> p (t o)", t=PACK))
+        gi_t = sb.tile([P, PACK], F32, name="gi_t")
+        nc.sync.dma_start(gi_t[:], gi.rearrange("(p t) o -> p (t o)", t=PACK))
+        n2_t = load_list("n2_t", n2)
+        n3_t = load_list("n3_t", n3)
+        n4_t = load_list("n4_t", n4)
+        n5_t = load_list("n5_t", n5)
+
+        a_win = [sb.tile([P, MEMBER_RUN + SPARE], F32, name=f"a_win{t}") for t in range(PACK)]
+        ex_win = [sb.tile([P, N + SPARE], F32, name=f"ex_win{t}", tag=f"ex_win{t}", align_bytes=64) for t in range(PACK)]
+        for win in a_win + ex_win:
+            nc.vector.memset(win[:, H:], 0.0)
+
+        def pick(name, table, dtype, index, tag):
+            picked = sb.tile([P, S], dtype, name=name + "_picked", tag=tag, align_bytes=64)
+            nc.vector.tensor_copy(picked[:], table[:].indirect(index[:]))
+            return picked
+
+        def deal(name, picked, dtype, t_lo, t_hi):
+            dealt = sb.tile([P, (t_hi - t_lo) * P], dtype, name=name, align_bytes=64)
+            nc.vector.tensor_copy(
+                dealt[:].rearrange("p (t m) -> p t m", m=P),
+                picked[:].rearrange("p (m t) -> p t m", t=PACK)[:, t_lo:t_hi, :],
+            )
+            return dealt
+
+        def rows_of(t):
+            return slice(t * P, (t + 1) * P)
+
+        xa_scales = deal("xa_scales", pick("xa_scales", x_scale_rows, U8, offs_t, "xa_scales_picked"), U8, 0, PACK)
+        wa_codes0 = sb.tile([P, WA_SPLIT], U32, name="wa_codes0", align_bytes=64)
+        wa_scales = sb.tile([P, H], U8, name="wa_scales", align_bytes=64)
+        wa_grouped0 = sb.tile([P, WA_SPLIT * PACK], BF16, name="wa_grouped0", align_bytes=64)
+        for u in range(2):
+            lo, hi = WA_PARTS[u]
+            weave(nc.scalar.copy, wa_grouped0[:, lo * PACK : hi * PACK], wa_raw[u][:])
+        quantize(wa_grouped0, wa_codes0[:], wa_scales[:, :WA_SPLIT])
+        xa_picked = pick("xa_words", x_word_table, U32, offs_t, "xa_words_picked")
+        xa_first = deal("xa_first", xa_picked, U32, 0, 1)
+        xa_others = deal("xa_others", xa_picked, U32, 1, PACK)
+        wa_codes1 = sb.tile([P, H - WA_SPLIT], U32, name="wa_codes1", tag="xa_words_picked", align_bytes=64)
+        quantize(
+            interleave(nc.scalar.copy, "wa_grouped1", wa_raw[2][:], H - WA_SPLIT), wa_codes1[:], wa_scales[:, WA_SPLIT:]
+        )
+        a_bank = [psum.tile([P, H], F32, name=f"a_bank{t}", tag=f"bank{t}") for t in range(PACK)]
+        a_rest = psum.tile([P, H - WA_SPLIT], F32, name="a_rest", tag=f"bank{PACK}")
+
+        def product_a(acc, t, lo, hi):
+            codes = wa_codes0[:, lo:hi] if hi <= WA_SPLIT else wa_codes1[:]
+            words = xa_first[:] if t == 0 else xa_others[:, rows_of(t - 1)]
+            product(acc, words, xa_scales[:, rows_of(t)], codes, wa_scales[:, lo:hi])
+
+        for lo, hi in ((0, 256), (256, WA_SPLIT)):
+            product_a(a_bank[0][:, lo:hi], 0, lo, hi)
+        product_a(a_rest[:], 0, WA_SPLIT, H)
+        nc.scalar.copy(a_win[0][:, :WA_SPLIT], a_bank[0][:, :WA_SPLIT])
+        nc.scalar.copy(a_win[0][:, WA_SPLIT:H], a_rest[:])
+        for t in range(1, PACK):
+            for lo, hi in ((0, 256), (256, WA_SPLIT), (WA_SPLIT, H)):
+                product_a(a_bank[t][:, lo:hi], t, lo, hi)
+            nc.vector.tensor_copy(a_win[t][:, :H], a_bank[t][:])
+
+        xb_words = deal("xb_words", pick("xb_words", x_word_table, U32, two_t, f"wa_raw{WA_SPLIT}"), U32, 0, PACK)
+        xb_scales = deal("xb_scales", pick("xb_scales", x_scale_rows, U8, two_t, f"wa_raw{WA_SPLIT}"), U8, 0, PACK)
+        wb_codes = sb.tile([P, N], U32, name="wb_codes", align_bytes=64)
+        wb_scales = sb.tile([P, N], U8, name="wb_scales", align_bytes=64)
+        quantize(interleave(nc.vector.tensor_copy, "wb_grouped", wb_raw[:], N, "wa_grouped1"), wb_codes[:], wb_scales[:])
+        b_bank = [psum.tile([P, N], F32, name=f"b_bank{t}", tag=f"bank{PACK + t}") for t in range(PACK)]
+        for t in range(PACK):
+            product(b_bank[t][:], xb_words[:, rows_of(t)], xb_scales[:, rows_of(t)], wb_codes[:], wb_scales[:])
+        bg_win = [sb.tile([P, N], F32, name=f"bg_win{t}") for t in range(PACK)]
+        for t in range(PACK):
+            nc.vector.tensor_scalar(bg_win[t][:], b_bank[t][:], gi_t[:, t : t + 1], None, ALU.mult)
+
+        member_sums = sb.tile([P, PACK * H], F32, name="member_sums")
+        z = sb.tile([P, PACK, H], F32, name="z")
+
+        def gather_members(t):
+            members = sb.tile([P, MEMBERS * H], F32, name=f"members{t}", tag=f"members{t}")
+            for lo in range(0, MEMBERS * H, MEMBER_RUN):
+                hi = lo + MEMBER_RUN
+                nc.scalar.activation(members[:, lo:hi], a_win[t][:].indirect(entries(n1_t, lo, hi)), ACT.Copy)
+            nc.vector.tensor_reduce(
+                member_sums[:, t * H : (t + 1) * H],
+                members[:].rearrange("p (j s) -> p j s", s=MEMBERS),
+                AX.X,
+                ALU.add,
+            )
+
+        def gate(t):
+            half_a = sb.tile([P, H], F32, name=f"half_a{t}")
+            nc.vector.tensor_scalar(half_a[:], a_win[t][:, :H], gt_t[:, t : t + 1], 0.5, ALU.mult, ALU.mult)
+            tanh = sb.tile([P, H], F32, name=f"tanh{t}")
+            nc.scalar.activation(tanh[:], member_sums[:, t * H : (t + 1) * H], ACT.Tanh, scale=0.5)
+            nc.vector.scalar_tensor_tensor(z[:, t, :], tanh[:], 1.0, half_a[:], ALU.add, ALU.mult)
+
+        for t in range(PACK):
+            gather_members(t)
+            if t > 0:
+                gate(t - 1)
+
+        ex_sum = sb.tile([P, PACK, N], F32, name="ex_sum")
+        for t in range(PACK):
+            nc.scalar.activation(ex_win[t][:, :N], b_bank[t][:], ACT.Exp)
+        gate(PACK - 1)
+        for t in range(PACK):
+            ex_other = member_sums[:, (PACK - 1 - t) * H : (PACK - t) * H]
+            nc.scalar.activation(ex_other, ex_win[t][:].indirect(n2_t[:]), ACT.Copy)
+            nc.vector.tensor_tensor(ex_sum[:, t, :], ex_win[t][:, :N], ex_other, ALU.add)
+        z_grouped = sb.tile([P, H * PACK], BF16, name="z_grouped", tag="ex_win0", align_bytes=64)
+        nc.vector.tensor_copy(
+            z_grouped[:].rearrange("p (s m t) -> p m t s", s=PACK, t=PACK),
+            z[:].rearrange("p t (m s) -> p m t s", s=PACK),
+        )
+        z_codes = sb.tile([P, H], U32, name="z_codes", align_bytes=64)
+        z_scales = sb.tile([P, H], U8, name="z_scales", align_bytes=64)
+        quantize(z_grouped, z_codes[:], z_scales[:])
+
+        last = Z2_CHUNKS[-1][0]
+        cv_bank = [psum.tile([P, last], F32, name=f"cv_bank{t}", tag=f"bank{t}") for t in range(PACK)]
+        cv_last = [psum.tile([P, N - last], F32, name=f"cv_last{t}", tag=f"bank{PACK + t}") for t in range(PACK)]
+        cv_win = [sb.tile([P, N], F32, name=f"cv_win{t}") for t in range(PACK)]
+        for c, (lo, hi) in enumerate(Z2_CHUNKS):
+            w = hi - lo
+            logs = sb.tile([P, PACK, w], F32, name=f"logs{lo}", tag=f"members{c}")
+            nc.scalar.activation(logs[:], ex_sum[:, :, lo:hi], ACT.Ln)
+            z2 = sb.tile([P, PACK, w], F32, name=f"z2_{lo}")
+            for t in range(PACK):
+                nc.scalar.activation(ex_sum[:, t, lo:hi], bg_win[t][:].indirect(entries(n3_t, lo, hi)), ACT.Copy)
+                nc.vector.scalar_tensor_tensor(
+                    z2[:, t, :], logs[:, t, :], gi_t[:, t : t + 1], ex_sum[:, t, lo:hi], ALU.mult, ALU.subtract
+                )
+            z2_codes = sb.tile([P, w], U32, name=f"z2_codes{lo}", align_bytes=64)
+            z2_scales = sb.tile([P, w], U8, name=f"z2_scales{lo}", align_bytes=64)
+            quantize(interleave(nc.vector.tensor_copy, f"z2_grouped{lo}", z2[:], w), z2_codes[:], z2_scales[:])
+            for t in range(PACK):
+                acc = cv_last[t][:] if lo == last else cv_bank[t][:, lo:hi]
+                product(acc, z_codes[:, rows_of(t)], z_scales[:, rows_of(t)], z2_codes[:], z2_scales[:])
+        for t in range(PACK):
+            nc.scalar.activation(cv_win[t][:, :last], cv_bank[t][:], ACT.Copy, scale=0.0625)
+        nc.scalar.activation(cv_win[0][:, last:], cv_last[0][:], ACT.Copy, scale=0.0625)
+        for t in range(1, PACK):
+            nc.vector.tensor_scalar(cv_win[t][:, last:], cv_last[t][:], 0.0625, None, ALU.mult)
+
+        out_rows = out_0.rearrange("(p t) c -> p t c", t=PACK)
+        out_words = out_1[0].rearrange("p n t -> p (n t)").bitcast(I32)
+        out_scales = sb.tile([P, N], U8, name="out_scales", align_bytes=64)
+        for lo, hi in OUT_CHUNKS:
+            w = hi - lo
+            y = sb.tile([P, PACK, w], F32, name=f"y{lo}")
+            for t in range(PACK):
+                first = sb.tile([P, w], F32, name=f"first{lo}_{t}")
+                second = sb.tile([P, w], F32, name=f"second{lo}_{t}")
+                larger = sb.tile([P, w], F32, name=f"larger{lo}_{t}")
+                nc.scalar.activation(first[:], cv_win[t][:].indirect(entries(n4_t, lo, hi)), ACT.Copy)
+                nc.scalar.activation(second[:], cv_win[t][:].indirect(entries(n5_t, lo, hi)), ACT.Copy)
+                nc.vector.tensor_tensor(larger[:], first[:], second[:], ALU.max)
+                nc.vector.scalar_tensor_tensor(y[:, t, :], cv_win[t][:, lo:hi], -0.75, larger[:], ALU.mult, ALU.add)
+            nc.sync.dma_start(out_rows[:, :, lo:hi], y[:])
+            y_codes = sb.tile([P, w], U32, name=f"y_codes{lo}", align_bytes=64)
+            quantize(interleave(nc.vector.tensor_copy, f"y_grouped{lo}", y[:], w), y_codes[:], out_scales[:, lo:hi])
+            nc.sync.dma_start(out_words[:, lo:hi], y_codes[:].bitcast(I32))
+        for q in range(4):
+            queue = nc.scalar if q % 2 == 0 else nc.sync
+            queue.dma_start(
+                out_2[0][4 * q : 4 * q + 4, :].bitcast(I32), out_scales[32 * q : 32 * q + 4, :].bitcast(I32)
+            )

@@ -22,9 +22,9 @@ LIST_ROWS = 16
 SPARE = 16
 MEMBER_RUN = 1024
 MEMBERS = 4
-WA_FIRST = 128
-WA_SPLIT = 384
-WA_PARTS = ((0, WA_FIRST), (WA_FIRST, WA_SPLIT), (WA_SPLIT, H))
+RUN = 8
+HALF = H // 2
+WA_SCALAR = 384
 Z2_CHUNKS = ((0, 256), (256, 384), (384, 512))
 OUT_CHUNKS = ((0, 256), (256, 384), (384, 512))
 
@@ -42,6 +42,11 @@ def tile_picked_mombgsumglseover_none_po_kernel(
         def load_list(name, src):
             tile = lists.tile(list(src.shape), U16, name=name)
             nc.sync.dma_start(tile[:], src)
+            return tile
+
+        def load_weights(name, src, t):
+            tile = sb.tile([P, 1], F32, name=name)
+            nc.sync.dma_start(tile[:], src.rearrange("(q t r) o -> t q r o", t=PACK, r=RUN)[t])
             return tile
 
         def entries(tile, lo, hi):
@@ -76,27 +81,21 @@ def tile_picked_mombgsumglseover_none_po_kernel(
         nc.vector.memset(x_scale_rows[:].bitcast(I32), 0)
         offs_t = load_list("offs_t", offs)
         wa_rows = wa.rearrange("(p j) c -> p j c", j=PACK)
-        wa_raw = [
-            sb.tile([P, PACK, hi - lo], F32, name=f"wa_raw{lo}", tag=f"wa_raw{lo}", align_bytes=64)
-            for lo, hi in WA_PARTS
-        ]
-        nc.sync.dma_start(wa_raw[0][:], wa_rows[:, :, :WA_FIRST])
+        wa_raw = [sb.tile([P, PACK, HALF], F32, name=f"wa_raw{u}") for u in range(2)]
+        nc.sync.dma_start(wa_raw[0][:], wa_rows[:, :, :HALF])
         for q in range(4):
             nc.sync.dma_start(
                 x_scale_rows[32 * q : 32 * q + 4, :].bitcast(I32), x_scales[0][4 * q : 4 * q + 4, :].bitcast(I32)
             )
-        nc.sync.dma_start(wa_raw[1][:], wa_rows[:, :, WA_FIRST:WA_SPLIT])
+        nc.sync.dma_start(wa_raw[1][:], wa_rows[:, :, HALF:])
         x_word_table = sb.tile([P, T], U32, name="x_word_table")
         nc.sync.dma_start(x_word_table[:].bitcast(I32), x_words[0].rearrange("p n t -> p (n t)").bitcast(I32))
-        nc.sync.dma_start(wa_raw[2][:], wa_rows[:, :, WA_SPLIT:])
         n1_t = load_list("n1_t", n1)
         wb_raw = sb.tile([P, PACK, N], F32, name="wb_raw")
         nc.sync.dma_start(wb_raw[:], wb.rearrange("(p j) c -> p j c", j=PACK))
         two_t = load_list("two_t", two)
-        gt_t = sb.tile([P, PACK], F32, name="gt_t")
-        nc.sync.dma_start(gt_t[:], gt.rearrange("(p t) o -> p (t o)", t=PACK))
-        gi_t = sb.tile([P, PACK], F32, name="gi_t")
-        nc.sync.dma_start(gi_t[:], gi.rearrange("(p t) o -> p (t o)", t=PACK))
+        gt_t = [load_weights(f"gt{t}", gt, t) for t in range(PACK)]
+        gi_t = [load_weights(f"gi{t}", gi, t) for t in range(PACK)]
         n2_t = load_list("n2_t", n2)
         n3_t = load_list("n3_t", n3)
         n4_t = load_list("n4_t", n4)
@@ -107,66 +106,55 @@ def tile_picked_mombgsumglseover_none_po_kernel(
         for win in a_win + ex_win:
             nc.vector.memset(win[:, H:], 0.0)
 
-        def pick(name, table, dtype, index, tag):
-            picked = sb.tile([P, S], dtype, name=name + "_picked", tag=tag, align_bytes=64)
-            nc.vector.tensor_copy(picked[:], table[:].indirect(index[:]))
-            return picked
-
-        def deal(name, picked, dtype, t_lo, t_hi):
-            dealt = sb.tile([P, (t_hi - t_lo) * P], dtype, name=name, align_bytes=64)
+        def pick_words(name, index):
+            words = sb.tile([P, S], U32, name=name, tag=name, align_bytes=64)
             nc.vector.tensor_copy(
-                dealt[:].rearrange("p (t m) -> p t m", m=P),
-                picked[:].rearrange("p (m t) -> p t m", t=PACK)[:, t_lo:t_hi, :],
+                words[:].rearrange("p (t q r) -> p q t r", t=PACK, r=RUN), x_word_table[:].indirect(index[:])
             )
-            return dealt
+            return words
+
+        def pick_scales(name, index, tag):
+            picked = sb.tile([P, S], U8, name=name + "_picked", tag=tag, align_bytes=64)
+            nc.vector.tensor_copy(picked[:], x_scale_rows[:].indirect(index[:]))
+            scales = sb.tile([P, S], U8, name=name, align_bytes=64)
+            nc.vector.tensor_copy(
+                scales[:].bitcast(I32).rearrange("p (t q r) -> p t q r", t=PACK, r=RUN // 4),
+                picked[:].bitcast(I32).rearrange("p (q t r) -> p t q r", t=PACK, r=RUN // 4),
+            )
+            return scales
 
         def rows_of(t):
             return slice(t * P, (t + 1) * P)
 
-        xa_scales = deal("xa_scales", pick("xa_scales", x_scale_rows, U8, offs_t, "xa_scales_picked"), U8, 0, PACK)
-        wa_codes0 = sb.tile([P, WA_SPLIT], U32, name="wa_codes0", align_bytes=64)
+        xa_scales = pick_scales("xa_scales", offs_t, "xa_scales_picked")
+        wa_grouped = sb.tile([P, H * PACK], BF16, name="wa_grouped", align_bytes=64)
+        weave(nc.scalar.copy, wa_grouped[:, : HALF * PACK], wa_raw[0][:])
+        weave(nc.scalar.copy, wa_grouped[:, HALF * PACK : WA_SCALAR * PACK], wa_raw[1][:, :, : WA_SCALAR - HALF])
+        weave(nc.vector.tensor_copy, wa_grouped[:, WA_SCALAR * PACK :], wa_raw[1][:, :, WA_SCALAR - HALF :])
+        wa_codes = sb.tile([P, H], U32, name="wa_codes", align_bytes=64)
         wa_scales = sb.tile([P, H], U8, name="wa_scales", align_bytes=64)
-        wa_grouped0 = sb.tile([P, WA_SPLIT * PACK], BF16, name="wa_grouped0", align_bytes=64)
-        for u in range(2):
-            lo, hi = WA_PARTS[u]
-            weave(nc.scalar.copy, wa_grouped0[:, lo * PACK : hi * PACK], wa_raw[u][:])
-        quantize(wa_grouped0, wa_codes0[:], wa_scales[:, :WA_SPLIT])
-        xa_picked = pick("xa_words", x_word_table, U32, offs_t, "xa_words_picked")
-        xa_first = deal("xa_first", xa_picked, U32, 0, 1)
-        xa_others = deal("xa_others", xa_picked, U32, 1, PACK)
-        wa_codes1 = sb.tile([P, H - WA_SPLIT], U32, name="wa_codes1", tag="xa_words_picked", align_bytes=64)
-        quantize(
-            interleave(nc.scalar.copy, "wa_grouped1", wa_raw[2][:], H - WA_SPLIT), wa_codes1[:], wa_scales[:, WA_SPLIT:]
-        )
+        quantize(wa_grouped, wa_codes[:], wa_scales[:])
+        xa_words = pick_words("xa_words", offs_t)
         a_bank = [psum.tile([P, H], F32, name=f"a_bank{t}", tag=f"bank{t}") for t in range(PACK)]
-        a_rest = psum.tile([P, H - WA_SPLIT], F32, name="a_rest", tag=f"bank{PACK}")
-
-        def product_a(acc, t, lo, hi):
-            codes = wa_codes0[:, lo:hi] if hi <= WA_SPLIT else wa_codes1[:]
-            words = xa_first[:] if t == 0 else xa_others[:, rows_of(t - 1)]
-            product(acc, words, xa_scales[:, rows_of(t)], codes, wa_scales[:, lo:hi])
-
-        for lo, hi in ((0, 256), (256, WA_SPLIT)):
-            product_a(a_bank[0][:, lo:hi], 0, lo, hi)
-        product_a(a_rest[:], 0, WA_SPLIT, H)
-        nc.scalar.copy(a_win[0][:, :WA_SPLIT], a_bank[0][:, :WA_SPLIT])
-        nc.scalar.copy(a_win[0][:, WA_SPLIT:H], a_rest[:])
+        a_rest = psum.tile([P, HALF], F32, name="a_rest", tag=f"bank{PACK}")
+        for acc, cols in ((a_bank[0][:, :HALF], slice(0, HALF)), (a_rest[:], slice(HALF, H))):
+            product(acc, xa_words[:, rows_of(0)], xa_scales[:, rows_of(0)], wa_codes[:, cols], wa_scales[:, cols])
+            nc.scalar.copy(a_win[0][:, cols], acc)
         for t in range(1, PACK):
-            for lo, hi in ((0, 256), (256, WA_SPLIT), (WA_SPLIT, H)):
-                product_a(a_bank[t][:, lo:hi], t, lo, hi)
+            product(a_bank[t][:], xa_words[:, rows_of(t)], xa_scales[:, rows_of(t)], wa_codes[:], wa_scales[:])
             nc.vector.tensor_copy(a_win[t][:, :H], a_bank[t][:])
 
-        xb_words = deal("xb_words", pick("xb_words", x_word_table, U32, two_t, f"wa_raw{WA_SPLIT}"), U32, 0, PACK)
-        xb_scales = deal("xb_scales", pick("xb_scales", x_scale_rows, U8, two_t, f"wa_raw{WA_SPLIT}"), U8, 0, PACK)
+        xb_words = pick_words("xb_words", two_t)
+        xb_scales = pick_scales("xb_scales", two_t, "xa_words")
         wb_codes = sb.tile([P, N], U32, name="wb_codes", align_bytes=64)
         wb_scales = sb.tile([P, N], U8, name="wb_scales", align_bytes=64)
-        quantize(interleave(nc.vector.tensor_copy, "wb_grouped", wb_raw[:], N, "wa_grouped1"), wb_codes[:], wb_scales[:])
+        quantize(interleave(nc.vector.tensor_copy, "wb_grouped", wb_raw[:], N), wb_codes[:], wb_scales[:])
         b_bank = [psum.tile([P, N], F32, name=f"b_bank{t}", tag=f"bank{PACK + t}") for t in range(PACK)]
         for t in range(PACK):
             product(b_bank[t][:], xb_words[:, rows_of(t)], xb_scales[:, rows_of(t)], wb_codes[:], wb_scales[:])
         bg_win = [sb.tile([P, N], F32, name=f"bg_win{t}") for t in range(PACK)]
         for t in range(PACK):
-            nc.vector.tensor_scalar(bg_win[t][:], b_bank[t][:], gi_t[:, t : t + 1], None, ALU.mult)
+            nc.vector.tensor_scalar(bg_win[t][:], b_bank[t][:], gi_t[t][:], None, ALU.mult)
 
         member_sums = sb.tile([P, PACK * H], F32, name="member_sums")
         z = sb.tile([P, PACK, H], F32, name="z")
@@ -183,27 +171,22 @@ def tile_picked_mombgsumglseover_none_po_kernel(
                 ALU.add,
             )
 
-        def gate(t):
-            half_a = sb.tile([P, H], F32, name=f"half_a{t}")
-            nc.vector.tensor_scalar(half_a[:], a_win[t][:, :H], gt_t[:, t : t + 1], 0.5, ALU.mult, ALU.mult)
-            tanh = sb.tile([P, H], F32, name=f"tanh{t}")
-            nc.scalar.activation(tanh[:], member_sums[:, t * H : (t + 1) * H], ACT.Tanh, scale=0.5)
-            nc.vector.scalar_tensor_tensor(z[:, t, :], tanh[:], 1.0, half_a[:], ALU.add, ALU.mult)
-
+        half_a = [sb.tile([P, H], F32, name=f"half_a{t}") for t in range(PACK)]
         for t in range(PACK):
             gather_members(t)
-            if t > 0:
-                gate(t - 1)
+            nc.vector.tensor_scalar(half_a[t][:], a_win[t][:, :H], gt_t[t][:], 0.5, ALU.mult, ALU.mult)
 
         ex_sum = sb.tile([P, PACK, N], F32, name="ex_sum")
         for t in range(PACK):
             nc.scalar.activation(ex_win[t][:, :N], b_bank[t][:], ACT.Exp)
-        gate(PACK - 1)
         for t in range(PACK):
-            ex_other = member_sums[:, (PACK - 1 - t) * H : (PACK - t) * H]
-            nc.scalar.activation(ex_other, ex_win[t][:].indirect(n2_t[:]), ACT.Copy)
-            nc.vector.tensor_tensor(ex_sum[:, t, :], ex_win[t][:, :N], ex_other, ALU.add)
-        z_grouped = sb.tile([P, H * PACK], BF16, name="z_grouped", tag="ex_win0", align_bytes=64)
+            sums = member_sums[:, t * H : (t + 1) * H]
+            tanh = sb.tile([P, H], F32, name=f"tanh{t}")
+            nc.scalar.activation(tanh[:], sums, ACT.Tanh, scale=0.5)
+            nc.scalar.activation(sums, ex_win[t][:].indirect(n2_t[:]), ACT.Copy)
+            nc.vector.tensor_tensor(ex_sum[:, t, :], ex_win[t][:, :N], sums, ALU.add)
+            nc.vector.scalar_tensor_tensor(z[:, t, :], tanh[:], 1.0, half_a[t][:], ALU.add, ALU.mult)
+        z_grouped = sb.tile([P, H * PACK], BF16, name="z_grouped", tag=f"ex_win{PACK - 1}", align_bytes=64)
         nc.vector.tensor_copy(
             z_grouped[:].rearrange("p (s m t) -> p m t s", s=PACK, t=PACK),
             z[:].rearrange("p t (m s) -> p m t s", s=PACK),
@@ -215,7 +198,6 @@ def tile_picked_mombgsumglseover_none_po_kernel(
         last = Z2_CHUNKS[-1][0]
         cv_bank = [psum.tile([P, last], F32, name=f"cv_bank{t}", tag=f"bank{t}") for t in range(PACK)]
         cv_last = [psum.tile([P, N - last], F32, name=f"cv_last{t}", tag=f"bank{PACK + t}") for t in range(PACK)]
-        cv_win = [sb.tile([P, N], F32, name=f"cv_win{t}") for t in range(PACK)]
         for c, (lo, hi) in enumerate(Z2_CHUNKS):
             w = hi - lo
             logs = sb.tile([P, PACK, w], F32, name=f"logs{lo}", tag=f"members{c}")
@@ -224,7 +206,7 @@ def tile_picked_mombgsumglseover_none_po_kernel(
             for t in range(PACK):
                 nc.scalar.activation(ex_sum[:, t, lo:hi], bg_win[t][:].indirect(entries(n3_t, lo, hi)), ACT.Copy)
                 nc.vector.scalar_tensor_tensor(
-                    z2[:, t, :], logs[:, t, :], gi_t[:, t : t + 1], ex_sum[:, t, lo:hi], ALU.mult, ALU.subtract
+                    z2[:, t, :], logs[:, t, :], gi_t[t][:], ex_sum[:, t, lo:hi], ALU.mult, ALU.subtract
                 )
             z2_codes = sb.tile([P, w], U32, name=f"z2_codes{lo}", align_bytes=64)
             z2_scales = sb.tile([P, w], U8, name=f"z2_scales{lo}", align_bytes=64)
@@ -232,11 +214,14 @@ def tile_picked_mombgsumglseover_none_po_kernel(
             for t in range(PACK):
                 acc = cv_last[t][:] if lo == last else cv_bank[t][:, lo:hi]
                 product(acc, z_codes[:, rows_of(t)], z_scales[:, rows_of(t)], z2_codes[:], z2_scales[:])
-        for t in range(PACK):
+        cv_win = [sb.tile([P, N], F32, name=f"cv_win{t}") for t in range(PACK - 1)]
+        cv_win.append(sb.tile([P, N], F32, name="cv_win3", tag=f"z2_grouped{last}", align_bytes=64))
+        for t in range(PACK - 1):
             nc.scalar.activation(cv_win[t][:, :last], cv_bank[t][:], ACT.Copy, scale=0.0625)
         nc.scalar.activation(cv_win[0][:, last:], cv_last[0][:], ACT.Copy, scale=0.0625)
         for t in range(1, PACK):
             nc.vector.tensor_scalar(cv_win[t][:, last:], cv_last[t][:], 0.0625, None, ALU.mult)
+        nc.vector.tensor_scalar(cv_win[PACK - 1][:, :last], cv_bank[PACK - 1][:], 0.0625, None, ALU.mult)
 
         out_rows = out_0.rearrange("(p t) c -> p t c", t=PACK)
         out_words = out_1[0].rearrange("p n t -> p (n t)").bitcast(I32)

@@ -83,10 +83,8 @@ def tile_picked_mombgsumglseover_none_po_kernel(
         wa_rows = wa.rearrange("(p j) c -> p j c", j=PACK)
         wa_raw = [sb.tile([P, PACK, HALF], F32, name=f"wa_raw{u}") for u in range(2)]
         nc.sync.dma_start(wa_raw[0][:], wa_rows[:, :, :HALF])
-        for q in range(4):
-            nc.sync.dma_start(
-                x_scale_rows[32 * q : 32 * q + 4, :].bitcast(I32), x_scales[0][4 * q : 4 * q + 4, :].bitcast(I32)
-            )
+        for r in range(4):
+            nc.sync.dma_start(x_scale_rows[r:P:32, :].bitcast(I32), x_scales[0][r:16:4, :].bitcast(I32))
         nc.sync.dma_start(wa_raw[1][:], wa_rows[:, :, HALF:])
         x_word_table = sb.tile([P, T], U32, name="x_word_table")
         nc.sync.dma_start(x_word_table[:].bitcast(I32), x_words[0].rearrange("p n t -> p (n t)").bitcast(I32))
@@ -102,7 +100,7 @@ def tile_picked_mombgsumglseover_none_po_kernel(
         n5_t = load_list("n5_t", n5)
 
         a_win = [sb.tile([P, MEMBER_RUN + SPARE], F32, name=f"a_win{t}") for t in range(PACK)]
-        ex_win = [sb.tile([P, N + SPARE], F32, name=f"ex_win{t}", tag=f"ex_win{t}", align_bytes=64) for t in range(PACK)]
+        ex_win = [sb.tile([P, N + SPARE], F32, name=f"ex_win{t}") for t in range(PACK)]
         for win in a_win + ex_win:
             nc.vector.memset(win[:, H:], 0.0)
 
@@ -156,37 +154,27 @@ def tile_picked_mombgsumglseover_none_po_kernel(
         for t in range(PACK):
             nc.vector.tensor_scalar(bg_win[t][:], b_bank[t][:], gi_t[t][:], None, ALU.mult)
 
-        member_sums = sb.tile([P, PACK * H], F32, name="member_sums")
         z = sb.tile([P, PACK, H], F32, name="z")
-
-        def gather_members(t):
-            members = sb.tile([P, MEMBERS * H], F32, name=f"members{t}", tag=f"members{t}")
-            for lo in range(0, MEMBERS * H, MEMBER_RUN):
-                hi = lo + MEMBER_RUN
-                nc.scalar.activation(members[:, lo:hi], a_win[t][:].indirect(entries(n1_t, lo, hi)), ACT.Copy)
-            nc.vector.tensor_reduce(
-                member_sums[:, t * H : (t + 1) * H],
-                members[:].rearrange("p (j s) -> p j s", s=MEMBERS),
-                AX.X,
-                ALU.add,
-            )
-
+        ex_other = sb.tile([P, PACK, N], F32, name="ex_other")
+        sums = [sb.tile([P, PACK, P], F32, name=f"sums{t}")[:] for t in range(PACK - 1)] + [ex_other[:, :, :P]]
         half_a = [sb.tile([P, H], F32, name=f"half_a{t}") for t in range(PACK)]
         for t in range(PACK):
-            gather_members(t)
+            members = sb.tile([P, MEMBERS * H], F32, name=f"members{t}", tag=f"members{t}")
+            for u in range(2):
+                lo, hi = u * MEMBER_RUN, (u + 1) * MEMBER_RUN
+                nc.scalar.activation(members[:, lo:hi], a_win[t][:].indirect(entries(n1_t, lo, hi)), ACT.Copy)
+                nc.vector.tensor_reduce(
+                    sums[t][:, 2 * u : 2 * u + 2, :],
+                    members[:, lo:hi].rearrange("p (g j s) -> p g j s", j=P, s=MEMBERS),
+                    AX.X,
+                    ALU.add,
+                )
             nc.vector.tensor_scalar(half_a[t][:], a_win[t][:, :H], gt_t[t][:], 0.5, ALU.mult, ALU.mult)
-
-        ex_sum = sb.tile([P, PACK, N], F32, name="ex_sum")
         for t in range(PACK):
-            nc.scalar.activation(ex_win[t][:, :N], b_bank[t][:], ACT.Exp)
-        for t in range(PACK):
-            sums = member_sums[:, t * H : (t + 1) * H]
             tanh = sb.tile([P, H], F32, name=f"tanh{t}")
-            nc.scalar.activation(tanh[:], sums, ACT.Tanh, scale=0.5)
-            nc.scalar.activation(sums, ex_win[t][:].indirect(n2_t[:]), ACT.Copy)
-            nc.vector.tensor_tensor(ex_sum[:, t, :], ex_win[t][:, :N], sums, ALU.add)
+            nc.scalar.activation(tanh[:].rearrange("p (g j) -> p g j", j=P), sums[t], ACT.Tanh, scale=0.5)
             nc.vector.scalar_tensor_tensor(z[:, t, :], tanh[:], 1.0, half_a[t][:], ALU.add, ALU.mult)
-        z_grouped = sb.tile([P, H * PACK], BF16, name="z_grouped", tag=f"ex_win{PACK - 1}", align_bytes=64)
+        z_grouped = sb.tile([P, H * PACK], BF16, name="z_grouped", align_bytes=64)
         nc.vector.tensor_copy(
             z_grouped[:].rearrange("p (s m t) -> p m t s", s=PACK, t=PACK),
             z[:].rearrange("p t (m s) -> p m t s", s=PACK),
@@ -194,6 +182,13 @@ def tile_picked_mombgsumglseover_none_po_kernel(
         z_codes = sb.tile([P, H], U32, name="z_codes", align_bytes=64)
         z_scales = sb.tile([P, H], U8, name="z_scales", align_bytes=64)
         quantize(z_grouped, z_codes[:], z_scales[:])
+
+        ex_sum = sb.tile([P, PACK, N], F32, name="ex_sum")
+        for t in range(PACK):
+            nc.scalar.activation(ex_win[t][:, :N], b_bank[t][:], ACT.Exp)
+        for t in range(PACK):
+            nc.scalar.activation(ex_other[:, t, :], ex_win[t][:].indirect(n2_t[:]), ACT.Copy)
+            nc.vector.tensor_tensor(ex_sum[:, t, :], ex_win[t][:, :N], ex_other[:, t, :], ALU.add)
 
         last = Z2_CHUNKS[-1][0]
         cv_bank = [psum.tile([P, last], F32, name=f"cv_bank{t}", tag=f"bank{t}") for t in range(PACK)]
@@ -241,8 +236,6 @@ def tile_picked_mombgsumglseover_none_po_kernel(
             y_codes = sb.tile([P, w], U32, name=f"y_codes{lo}", align_bytes=64)
             quantize(interleave(nc.vector.tensor_copy, f"y_grouped{lo}", y[:], w), y_codes[:], out_scales[:, lo:hi])
             nc.sync.dma_start(out_words[:, lo:hi], y_codes[:].bitcast(I32))
-        for q in range(4):
-            queue = nc.scalar if q % 2 == 0 else nc.sync
-            queue.dma_start(
-                out_2[0][4 * q : 4 * q + 4, :].bitcast(I32), out_scales[32 * q : 32 * q + 4, :].bitcast(I32)
-            )
+        for r in range(4):
+            queue = nc.scalar if r % 2 == 0 else nc.sync
+            queue.dma_start(out_2[0][r:16:4, :].bitcast(I32), out_scales[r:P:32, :].bitcast(I32))

from contextlib import ExitStack

import concourse.mybir as mybir

K, T, S, N, H = 512, 2048, 512, 512, 512
FLOPS = 3 * 2 * 512 * 512 * 512

F32 = mybir.dt.float32
BF16 = mybir.dt.bfloat16
I32 = mybir.dt.int32
U32 = mybir.dt.uint32
U16 = mybir.dt.uint16
U8 = mybir.dt.uint8
FP8X4 = mybir.dt.float8_e4m3fn_x4
ACT = mybir.ActivationFunctionType
ALU = mybir.AluOpType
AX = mybir.AxisListType

P = 128
PACK = 4
LIST_ROWS = 16
SPARE = 16
MEMBER_RUN = 1024
MEMBERS = 4
RUN = 8
HALF = H // 2
WA_SCALAR = 384
Z2_CHUNKS = ((0, 256), (256, 384), (384, 512))
OUT_CHUNKS = ((0, 256), (256, 384), (384, 512))


def tile_picked_mombgsumglseover_none_po_kernel(
    tc, x_words, x_scales, wa, wb, gt, gi, offs, two, n1, n2, n3, n4, n5, out_0, out_1, out_2
):
    nc = tc.nc

    with ExitStack() as ctx:
        lists = ctx.enter_context(tc.tile_pool(name="lists", bufs=1))
        sb = ctx.enter_context(tc.tile_pool(name="sb", bufs=1))
        psum = ctx.enter_context(tc.psum_pool(name="psum", bufs=1))

        def load_list(name, src):
            tile = lists.tile(list(src.shape), U16, name=name)
            nc.sync.dma_start(tile[:], src)
            return tile

        def load_weights(name, src, t):
            tile = sb.tile([P, 1], F32, name=name)
            nc.sync.dma_start(tile[:], src.rearrange("(q t r) o -> t q r o", t=PACK, r=RUN)[t])
            return tile

        def entries(tile, lo, hi):
            return tile[:, lo // LIST_ROWS : hi // LIST_ROWS]

        def weave(engine_copy, grouped, planes):
            engine_copy(
                grouped.rearrange("p (c i t) -> p c t i", i=4, t=PACK),
                planes.rearrange("p t (c i) -> p c t i", i=4),
            )

        def interleave(engine_copy, name, planes, width, tag=None):
            grouped = sb.tile([P, width * PACK], BF16, name=name, tag=tag or name, align_bytes=64)
            weave(engine_copy, grouped[:], planes)
            return grouped

        def quantize(grouped, codes, scales):
            nc.vector.quantize_mx(out=codes.bitcast(FP8X4), scales=scales, in_=grouped[:])

        def product(out, lhs_codes, lhs_scales, rhs_codes, rhs_scales):
            nc.tensor.matmul_mx(
                out=out,
                lhsT=lhs_codes.bitcast(FP8X4),
                lhsT_scale=lhs_scales,
                rhs=rhs_codes.bitcast(FP8X4),
                rhs_scale=rhs_scales,
                start=True,
                stop=True,
            )

        x_scale_rows = sb.tile([P, T], U8, name="x_scale_rows")
        nc.vector.memset(x_scale_rows[:].bitcast(I32), 0)
        offs_t = load_list("offs_t", offs)
        wa_rows = wa.rearrange("(p j) c -> p j c", j=PACK)
        wa_raw = [sb.tile([P, PACK, HALF], F32, name=f"wa_raw{u}") for u in range(2)]
        nc.sync.dma_start(wa_raw[0][:], wa_rows[:, :, :HALF])
        for r in range(4):
            nc.sync.dma_start(x_scale_rows[r:P:32, :].bitcast(I32), x_scales[0][r:16:4, :].bitcast(I32))
        nc.sync.dma_start(wa_raw[1][:], wa_rows[:, :, HALF:])
        x_word_table = sb.tile([P, T], U32, name="x_word_table")
        nc.sync.dma_start(x_word_table[:].bitcast(I32), x_words[0].rearrange("p n t -> p (n t)").bitcast(I32))
        n1_t = load_list("n1_t", n1)
        wb_raw = sb.tile([P, PACK, N], F32, name="wb_raw")
        nc.sync.dma_start(wb_raw[:], wb.rearrange("(p j) c -> p j c", j=PACK))
        two_t = load_list("two_t", two)
        gt_t = [load_weights(f"gt{t}", gt, t) for t in range(PACK)]
        gi_t = [load_weights(f"gi{t}", gi, t) for t in range(PACK)]
        n2_t = load_list("n2_t", n2)
        n3_t = load_list("n3_t", n3)
        n4_t = load_list("n4_t", n4)
        n5_t = load_list("n5_t", n5)

        a_win = [sb.tile([P, MEMBER_RUN + SPARE], F32, name=f"a_win{t}") for t in range(PACK)]
        ex_win = [sb.tile([P, N + SPARE], F32, name=f"ex_win{t}") for t in range(PACK)]
        for win in a_win + ex_win:
            nc.vector.memset(win[:, H:], 0.0)

        def pick_words(name, index):
            words = sb.tile([P, S], U32, name=name, tag=name, align_bytes=64)
            nc.vector.tensor_copy(
                words[:].rearrange("p (t q r) -> p q t r", t=PACK, r=RUN), x_word_table[:].indirect(index[:])
            )
            return words

        def pick_scales(name, index, tag):
            picked = sb.tile([P, S], U8, name=name + "_picked", tag=tag, align_bytes=64)
            nc.vector.tensor_copy(picked[:], x_scale_rows[:].indirect(index[:]))
            scales = sb.tile([P, S], U8, name=name, align_bytes=64)
            nc.vector.tensor_copy(
                scales[:].bitcast(I32).rearrange("p (t q r) -> p t q r", t=PACK, r=RUN // 4),
                picked[:].bitcast(I32).rearrange("p (q t r) -> p t q r", t=PACK, r=RUN // 4),
            )
            return scales

        def rows_of(t):
            return slice(t * P, (t + 1) * P)

        xa_scales = pick_scales("xa_scales", offs_t, "xa_scales_picked")
        wa_grouped = sb.tile([P, H * PACK], BF16, name="wa_grouped", align_bytes=64)
        weave(nc.scalar.copy, wa_grouped[:, : HALF * PACK], wa_raw[0][:])
        weave(nc.scalar.copy, wa_grouped[:, HALF * PACK : WA_SCALAR * PACK], wa_raw[1][:, :, : WA_SCALAR - HALF])
        weave(nc.vector.tensor_copy, wa_grouped[:, WA_SCALAR * PACK :], wa_raw[1][:, :, WA_SCALAR - HALF :])
        wa_codes = sb.tile([P, H], U32, name="wa_codes", align_bytes=64)
        wa_scales = sb.tile([P, H], U8, name="wa_scales", align_bytes=64)
        quantize(wa_grouped, wa_codes[:], wa_scales[:])
        xa_words = pick_words("xa_words", offs_t)
        a_bank = [psum.tile([P, H], F32, name=f"a_bank{t}", tag=f"bank{t}") for t in range(PACK)]
        a_rest = psum.tile([P, HALF], F32, name="a_rest", tag=f"bank{PACK}")
        for acc, cols in ((a_bank[0][:, :HALF], slice(0, HALF)), (a_rest[:], slice(HALF, H))):
            product(acc, xa_words[:, rows_of(0)], xa_scales[:, rows_of(0)], wa_codes[:, cols], wa_scales[:, cols])
            nc.scalar.copy(a_win[0][:, cols], acc)
        for t in range(1, PACK):
            product(a_bank[t][:], xa_words[:, rows_of(t)], xa_scales[:, rows_of(t)], wa_codes[:], wa_scales[:])
            nc.vector.tensor_copy(a_win[t][:, :H], a_bank[t][:])

        xb_words = pick_words("xb_words", two_t)
        xb_scales = pick_scales("xb_scales", two_t, "xa_words")
        wb_codes = sb.tile([P, N], U32, name="wb_codes", align_bytes=64)
        wb_scales = sb.tile([P, N], U8, name="wb_scales", align_bytes=64)
        quantize(interleave(nc.vector.tensor_copy, "wb_grouped", wb_raw[:], N), wb_codes[:], wb_scales[:])
        b_bank = [psum.tile([P, N], F32, name=f"b_bank{t}", tag=f"bank{PACK + t}") for t in range(PACK)]
        for t in range(PACK):
            product(b_bank[t][:], xb_words[:, rows_of(t)], xb_scales[:, rows_of(t)], wb_codes[:], wb_scales[:])
        bg_win = [sb.tile([P, N], F32, name=f"bg_win{t}") for t in range(PACK)]
        for t in range(PACK):
            nc.vector.tensor_scalar(bg_win[t][:], b_bank[t][:], gi_t[t][:], None, ALU.mult)

        z = sb.tile([P, PACK, H], F32, name="z")
        ex_other = sb.tile([P, PACK, N], F32, name="ex_other")
        sums = [sb.tile([P, PACK, P], F32, name=f"sums{t}")[:] for t in range(PACK - 1)] + [ex_other[:, :, :P]]
        half_a = [sb.tile([P, H], F32, name=f"half_a{t}") for t in range(PACK)]
        for t in range(PACK):
            members = sb.tile([P, MEMBERS * H], F32, name=f"members{t}", tag=f"members{t}")
            for u in range(2):
                lo, hi = u * MEMBER_RUN, (u + 1) * MEMBER_RUN
                nc.scalar.activation(members[:, lo:hi], a_win[t][:].indirect(entries(n1_t, lo, hi)), ACT.Copy)
                nc.vector.tensor_reduce(
                    sums[t][:, 2 * u : 2 * u + 2, :],
                    members[:, lo:hi].rearrange("p (g j s) -> p g j s", j=P, s=MEMBERS),
                    AX.X,
                    ALU.add,
                )
            nc.vector.tensor_scalar(half_a[t][:], a_win[t][:, :H], gt_t[t][:], 0.5, ALU.mult, ALU.mult)
        for t in range(PACK):
            tanh = sb.tile([P, H], F32, name=f"tanh{t}")
            nc.scalar.activation(tanh[:].rearrange("p (g j) -> p g j", j=P), sums[t], ACT.Tanh, scale=0.5)
            nc.vector.scalar_tensor_tensor(z[:, t, :], tanh[:], 1.0, half_a[t][:], ALU.add, ALU.mult)
        z_grouped = sb.tile([P, H * PACK], BF16, name="z_grouped", align_bytes=64)
        nc.vector.tensor_copy(
            z_grouped[:].rearrange("p (s m t) -> p m t s", s=PACK, t=PACK),
            z[:].rearrange("p t (m s) -> p m t s", s=PACK),
        )
        z_codes = sb.tile([P, H], U32, name="z_codes", align_bytes=64)
        z_scales = sb.tile([P, H], U8, name="z_scales", align_bytes=64)
        quantize(z_grouped, z_codes[:], z_scales[:])

        ex_sum = sb.tile([P, PACK, N], F32, name="ex_sum")
        for t in range(PACK):
            nc.scalar.activation(ex_win[t][:, :N], b_bank[t][:], ACT.Exp)
        for t in range(PACK):
            nc.scalar.activation(ex_other[:, t, :], ex_win[t][:].indirect(n2_t[:]), ACT.Copy)
            nc.vector.tensor_tensor(ex_sum[:, t, :], ex_win[t][:, :N], ex_other[:, t, :], ALU.add)

        last = Z2_CHUNKS[-1][0]
        cv_bank = [psum.tile([P, last], F32, name=f"cv_bank{t}", tag=f"bank{t}") for t in range(PACK)]
        cv_last = [psum.tile([P, N - last], F32, name=f"cv_last{t}", tag=f"bank{PACK + t}") for t in range(PACK)]
        for c, (lo, hi) in enumerate(Z2_CHUNKS):
            w = hi - lo
            logs = sb.tile([P, PACK, w], F32, name=f"logs{lo}", tag=f"members{c}")
            nc.scalar.activation(logs[:], ex_sum[:, :, lo:hi], ACT.Ln)
            z2 = sb.tile([P, PACK, w], F32, name=f"z2_{lo}")
            for t in range(PACK):
                nc.scalar.activation(ex_sum[:, t, lo:hi], bg_win[t][:].indirect(entries(n3_t, lo, hi)), ACT.Copy)
                nc.vector.scalar_tensor_tensor(
                    z2[:, t, :], logs[:, t, :], gi_t[t][:], ex_sum[:, t, lo:hi], ALU.mult, ALU.subtract
                )
            z2_codes = sb.tile([P, w], U32, name=f"z2_codes{lo}", align_bytes=64)
            z2_scales = sb.tile([P, w], U8, name=f"z2_scales{lo}", align_bytes=64)
            quantize(interleave(nc.vector.tensor_copy, f"z2_grouped{lo}", z2[:], w), z2_codes[:], z2_scales[:])
            for t in range(PACK):
                acc = cv_last[t][:] if lo == last else cv_bank[t][:, lo:hi]
                product(acc, z_codes[:, rows_of(t)], z_scales[:, rows_of(t)], z2_codes[:], z2_scales[:])
        cv_win = [sb.tile([P, N], F32, name=f"cv_win{t}") for t in range(PACK - 1)]
        cv_win.append(sb.tile([P, N], F32, name="cv_win3", tag=f"z2_grouped{last}", align_bytes=64))
        for t in range(PACK - 1):
            nc.scalar.activation(cv_win[t][:, :last], cv_bank[t][:], ACT.Copy, scale=0.0625)
        nc.scalar.activation(cv_win[0][:, last:], cv_last[0][:], ACT.Copy, scale=0.0625)
        for t in range(1, PACK):
            nc.vector.tensor_scalar(cv_win[t][:, last:], cv_last[t][:], 0.0625, None, ALU.mult)
        nc.vector.tensor_scalar(cv_win[PACK - 1][:, :last], cv_bank[PACK - 1][:], 0.0625, None, ALU.mult)

        out_rows = out_0.rearrange("(p t) c -> p t c", t=PACK)
        out_words = out_1[0].rearrange("p n t -> p (n t)").bitcast(I32)
        out_scales = sb.tile([P, N], U8, name="out_scales", align_bytes=64)
        for lo, hi in OUT_CHUNKS:
            w = hi - lo
            y = sb.tile([P, PACK, w], F32, name=f"y{lo}")
            for t in range(PACK):
                first = sb.tile([P, w], F32, name=f"first{lo}_{t}")
                second = sb.tile([P, w], F32, name=f"second{lo}_{t}")
                larger = sb.tile([P, w], F32, name=f"larger{lo}_{t}")
                nc.scalar.activation(first[:], cv_win[t][:].indirect(entries(n4_t, lo, hi)), ACT.Copy)
                nc.scalar.activation(second[:], cv_win[t][:].indirect(entries(n5_t, lo, hi)), ACT.Copy)
                nc.vector.tensor_tensor(larger[:], first[:], second[:], ALU.max)
                nc.vector.scalar_tensor_tensor(y[:, t, :], cv_win[t][:, lo:hi], -0.75, larger[:], ALU.mult, ALU.add)
            nc.sync.dma_start(out_rows[:, :, lo:hi], y[:])
            y_codes = sb.tile([P, w], U32, name=f"y_codes{lo}", align_bytes=64)
            quantize(interleave(nc.vector.tensor_copy, f"y_grouped{lo}", y[:], w), y_codes[:], out_scales[:, lo:hi])
            nc.sync.dma_start(out_words[:, lo:hi], y_codes[:].bitcast(I32))
        for r in range(4):
            queue = nc.scalar if r % 2 == 0 else nc.sync
            queue.dma_start(out_2[0][r:16:4, :].bitcast(I32), out_scales[r:P:32, :].bitcast(I32))
